import numpy as np
import ml_dtypes


def mxq(x, axis, fmt="e4m3"):
    dtype, down = {"e4m3": (ml_dtypes.float8_e4m3fn, 7), "e5m2": (ml_dtypes.float8_e5m2, 14)}[fmt]
    v = np.moveaxis(np.asarray(x, np.float32).astype(ml_dtypes.bfloat16).astype(np.float64), axis, -1)
    blocks = v.reshape(v.shape[:-1] + (-1, 32))
    amax = np.abs(blocks).max(-1, keepdims=True)
    byte = np.maximum(np.where(amax > 0, np.frexp(amax)[1] - 1 + 127, 0) - down, 1)
    scale = np.exp2(byte - 127.0)
    codes = (blocks / scale).astype(np.float32).astype(dtype).astype(np.float64)
    return np.moveaxis((codes * scale).reshape(v.shape), -1, axis)


WIDE = False


def mx_kscale(k):
    if not WIDE:
        return np.ones(k)
    levels = np.array([10, -10, 5, -5, 0])
    if k % 512:
        return np.exp2(np.random.permutation(np.resize(levels, k // 32))).repeat(32)
    a = np.empty((k // 512, 16))
    for p in range(k // 512):
        a[p, :8] = np.random.permutation(np.resize(levels, 8))
        for g in range(8):
            far = levels[np.abs(levels - a[p, g]) >= 10]
            a[p, g + 8] = far[np.random.randint(len(far))]
    return np.exp2(a.ravel()).repeat(32)


def f64(x):
    return np.asarray(x).astype(np.float64)


def striped(idx):
    return np.tile(idx.reshape(-1, 16).T, (8, 1)).astype(np.uint16)


def unstriped(offs):
    return offs[:16].T.reshape(-1).astype(np.int64)


def pack_weight(w):
    k, n = w.shape
    w = f64(np.asarray(w, np.float32).astype(ml_dtypes.bfloat16)).reshape(k // 32, 32, n)
    amax = np.abs(w).max(1)
    byte = np.clip(np.where(amax > 0, np.frexp(amax)[1] - 1 + 127 - 7, 1), 1, 254)
    scaled = (w * np.exp2(127.0 - byte)[:, None, :]).reshape(k, n).astype(np.float32)
    words = np.ascontiguousarray(scaled.reshape(k // 512, 128, 4, n).transpose(0, 1, 3, 2)).astype(ml_dtypes.float8_e4m3fn).view(np.uint8)
    return words, np.ascontiguousarray(byte.astype(np.uint8).reshape(k // 512, 16, n))


def unpack_weight(words, scales):
    g, p, n, _ = words.shape
    vals = np.ascontiguousarray(words).view(ml_dtypes.float8_e4m3fn).astype(np.float64) * np.repeat(np.exp2(scales.astype(np.float64) - 127.0), 8, axis=1)[..., None]
    return vals.transpose(0, 1, 3, 2).reshape(g * 512, n)


E2M1 = np.array([0.0, 0.5, 1.0, 1.5, 2.0, 3.0, 4.0, 6.0, -0.0, -0.5, -1.0, -1.5, -2.0, -3.0, -4.0, -6.0])


def pack_fp4(w):
    k, n = w.shape
    w = f64(np.asarray(w, np.float32).astype(ml_dtypes.bfloat16)).reshape(k // 32, 32, n)
    amax = np.abs(w).max(1)
    mant, ex = np.frexp(amax / 6.0)
    byte = np.clip(np.where(amax > 0, np.where(mant > 0.5, ex, ex - 1) + 127, 1), 1, 254)
    scaled = (w * np.exp2(127.0 - byte)[:, None, :]).reshape(k, n).astype(np.float32)
    c = np.ascontiguousarray(scaled.reshape(k // 512, 128, 4, n).transpose(0, 1, 3, 2)).astype(ml_dtypes.float4_e2m1fn).view(np.uint8) & 0xF
    words = (c[..., 0::2] | (c[..., 1::2] << 4)).reshape(k // 512, 128, 2 * n)
    return np.ascontiguousarray(words), np.ascontiguousarray(byte.astype(np.uint8).reshape(k // 512, 16, n))


def unpack_fp4(words, scales):
    g, _, n = scales.shape
    words = np.ascontiguousarray(words).reshape(g, 128, n, 2)
    nib = np.empty((g, 128, n, 4), np.uint8)
    nib[..., 0::2] = words & 0xF
    nib[..., 1::2] = words >> 4
    vals = E2M1[nib] * np.repeat(np.exp2(scales.astype(np.float64) - 127.0), 8, axis=1)[..., None]
    return vals.transpose(0, 1, 3, 2).reshape(g * 512, n)


K, T, S, N, H = 512, 2048, 512, 128, 512


def setup_inputs():
    n = np.random.standard_normal
    s = mx_kscale(K)[:, None]
    u = mx_kscale(H)
    packed_xT = pack_weight(n((K, T)) * s)
    packed_w1 = pack_fp4(n((K, H)) / np.sqrt(K) / s)
    packed_w2 = pack_fp4(n((K, H)) / np.sqrt(K) / s)
    packed_w3 = pack_fp4(n((K, H)) / np.sqrt(K) / s)
    packed_w4 = pack_fp4(n((H, N)) / np.sqrt(H) / u[:, None])
    return {
        "x_words": packed_xT[0],
        "x_scales": packed_xT[1],
        "w1_words": packed_w1[0],
        "w1_scales": packed_w1[1],
        "w2_words": packed_w2[0],
        "w2_scales": packed_w2[1],
        "w3_words": packed_w3[0],
        "w3_scales": packed_w3[1],
        "unit": (np.random.uniform(0.6, 1.4, (H, 1)) * u[:, None]).astype(np.float32),
        "w4_words": packed_w4[0],
        "w4_scales": packed_w4[1],
        "offs": striped(np.random.permutation(T)[:S]),
        "prev": striped(np.random.permutation(S)),
    }


def reference(x_words, x_scales, w1_words, w1_scales, w2_words, w2_scales, w3_words, w3_scales, unit, w4_words, w4_scales, offs, prev):
    xq = unpack_weight(x_words, x_scales)[:, unstriped(offs)]
    vmx = unpack_fp4(w3_words, w3_scales).T @ xq
    vmax = np.log(np.exp(vmx) + 1.0)
    cl = unpack_fp4(w1_words, w1_scales).T @ xq
    conc = np.log(np.exp(cl) + 1.0)
    vd = unpack_fp4(w2_words, w2_scales).T @ xq
    km = np.log(np.exp(vd) + 1.0) + 0.3
    rate = (vmax * conc) / (km + conc)
    cp = conc[:, unstriped(prev)]
    inh = -1.0 * (cp / (conc[:, unstriped(prev)] + km)) + 1.0
    mp = rate[:, unstriped(prev)] * inh
    hid = f64(unit) * (rate - (0.6 * mp))
    return unpack_fp4(w4_words, w4_scales).T @ mxq(hid, 0, "e4m3")

@@ -1,0 +1,199 @@
+from contextlib import ExitStack
+
+import concourse.mybir as mybir
+
+F32 = mybir.dt.float32
+BF16 = mybir.dt.bfloat16
+I32 = mybir.dt.int32
+U32 = mybir.dt.uint32
+U16 = mybir.dt.uint16
+U8 = mybir.dt.uint8
+FP8X4 = mybir.dt.float8_e4m3fn_x4
+FP4X4 = mybir.dt.float4_e2m1fn_x4
+ALU = mybir.AluOpType
+ACT = mybir.ActivationFunctionType
+
+P = 128
+PACK = 4
+K, T, S, N, H = 512, 2048, 512, 128, 512
+CHUNK = 128
+TINY = 1e-18
+FLOPS = 2 * K * H * S * 3 + 2 * H * N * S
+
+
+def tile_picked_yumfpk_wash_p_kernel(
+    tc, x_words, x_scales, w1_words, w1_scales, w2_words, w2_scales, w3_words, w3_scales,
+    unit, w4_words, w4_scales, offs, prev, out,
+):
+    nc = tc.nc
+    with ExitStack() as ctx:
+        held = ctx.enter_context(tc.tile_pool(name="held", bufs=1))
+        psum = ctx.enter_context(tc.psum_pool(name="psum", bufs=1))
+
+        def tiles(name, count, shape, dtype):
+            return [held.tile(shape, dtype, name="%s%d" % (name, i), align_bytes=64) for i in range(count)]
+
+        def load_scale_rows(dst, src, last_queue=nc.sync):
+            for q in range(4):
+                queue = last_queue if q == 3 else nc.sync
+                queue.dma_start(dst[32 * q : 32 * q + 4, :].bitcast(I32), src[0, 4 * q : 4 * q + 4, :].bitcast(I32))
+
+        offs_list = held.tile([P, S // 16], U16, name="offs_list")
+        prev_list = held.tile([P, S // 16], U16, name="prev_list")
+        x_table = held.tile([P, T], U32, name="x_table", align_bytes=64)
+        x_table_scales = held.tile([P, T], U8, name="x_table_scales", tag="scales_then_gain", align_bytes=64)
+        w_raw_scales = held.tile([P, 3 * H + N], U8, name="w_raw_scales", align_bytes=64)
+
+        nc.vector.memset(x_table_scales[:].bitcast(I32), 0)
+        nc.gpsimd.memset(w_raw_scales[:].bitcast(I32), 0)
+
+        words_in = (w1_words, w3_words, w2_words)
+        scales_in = (w1_scales, w3_scales, w2_scales)
+        def load_words(name, src):
+            raw = held.tile([P, src.shape[2]], U8, name=name, tag="w_raw", align_bytes=64)
+            nc.sync.dma_start(raw[:].bitcast(I32), src[0].bitcast(I32))
+            return raw
+
+        nc.sync.dma_start(offs_list[:], offs)
+        nc.sync.dma_start(prev_list[:], prev)
+        first_raw = load_words("w_raw0", words_in[0])
+        nc.sync.dma_start(x_table[:].bitcast(I32), x_words[0].rearrange("p n t -> p (n t)").bitcast(I32))
+        load_scale_rows(x_table_scales[:], x_scales)
+        load_scale_rows(w_raw_scales[:, :H], scales_in[0], last_queue=nc.gpsimd)
+        for i in (1, 2):
+            load_scale_rows(w_raw_scales[:, i * H : (i + 1) * H], scales_in[i])
+        load_scale_rows(w_raw_scales[:, 3 * H :], w4_scales)
+
+        w_codes = tiles("w_codes", 3, [P, 2 * H], U8)
+        w_scales = tiles("w_scales", 3, [P, H], U8)
+
+        def deal_words(i, raw):
+            nc.vector.tensor_copy(
+                w_codes[i][:].rearrange("p (t m b) -> p t m b", t=PACK, b=2),
+                raw[:].rearrange("p (m t b) -> p t m b", t=PACK, b=2),
+            )
+
+        def deal_scales(i):
+            nc.vector.tensor_copy(
+                w_scales[i][:].rearrange("p (t m) -> p t m", t=PACK),
+                w_raw_scales[:, i * H : (i + 1) * H].rearrange("p (m t) -> p t m", t=PACK),
+            )
+
+        x_codes = held.tile([P, S], U32, name="x_codes", align_bytes=64)
+        x_picked_scales = held.tile([P, S], U8, name="x_picked_scales", align_bytes=64)
+        deal_words(0, first_raw)
+        nc.vector.tensor_copy(x_picked_scales[:], x_table_scales[:].indirect(offs_list[:]))
+        nc.vector.tensor_copy(x_codes[:], x_table[:].indirect(offs_list[:]))
+        deal_scales(0)
+        for i in (1, 2):
+            deal_words(i, load_words("w_raw%d" % i, words_in[i]))
+            deal_scales(i)
+        w4_codes = load_words("w4_codes", w4_words)
+        gain = held.tile([P, PACK], F32, name="gain", tag="scales_then_gain", align_bytes=64)
+        nc.sync.dma_start(gain[:], unit.rearrange("(p t) o -> p (t o)", t=PACK))
+
+        def product(i, t, tag):
+            bank = psum.tile([P, S], F32, name="pre%d_%d" % (i, t), tag="%s%d" % (tag, t))
+            nc.tensor.matmul_mx(
+                out=bank[:],
+                lhsT=w_codes[i][:, 2 * P * t : 2 * P * (t + 1)].bitcast(FP4X4),
+                lhsT_scale=w_scales[i][:, P * t : P * (t + 1)],
+                rhs=x_codes[:].bitcast(FP8X4),
+                rhs_scale=x_picked_scales[:],
+                start=True,
+                stop=True,
+            )
+            return bank
+
+        pair = tiles("pair", PACK, [P, 2 * S], F32)
+        conc_win = tiles("conc_win", PACK, [P, 2 * S], F32)
+        sig_v = tiles("sig_v", PACK, [P, S], F32)
+        log_km = tiles("log_km", PACK, [P, S], F32)
+        sat_logit = tiles("sat_logit", PACK, [P, S], F32)
+        inh_logit = held.tile([P, PACK, S], F32, name="inh_logit", align_bytes=64)
+        rate = held.tile([P, PACK, S], F32, name="rate", align_bytes=64)
+
+        for t in range(PACK):
+            bank = product(0, t, "a")
+            nc.scalar.activation(pair[t][:, :S], bank[:], ACT.Sigmoid, scale=-1.0)
+            nc.vector.tensor_scalar_max(conc_win[t][:, S:], bank[:], TINY)
+        vmx = []
+        for t in range(PACK):
+            vmx.append(product(1, t, "b"))
+            nc.scalar.activation(sig_v[t][:], vmx[t][:], ACT.Sigmoid, scale=-1.0)
+        vd = []
+        for t in range(PACK):
+            vd.append(product(2, t, "a"))
+            nc.scalar.activation(pair[t][:, S:], vd[t][:], ACT.Sigmoid, scale=-1.0)
+
+        def softplus_pair(t):
+            nc.scalar.activation(pair[t][:], pair[t][:], ACT.Ln, bias=TINY)
+            nc.vector.scalar_tensor_tensor(conc_win[t][:, S:], pair[t][:, :S], -1.0, conc_win[t][:, S:], ALU.mult, ALU.max)
+            nc.vector.scalar_tensor_tensor(pair[t][:, S:], pair[t][:, S:], -1.0, vd[t][:], ALU.mult, ALU.max)
+
+        def logs(t):
+            nc.scalar.activation(conc_win[t][:, :S], conc_win[t][:, S:], ACT.Ln)
+            nc.scalar.activation(log_km[t][:], pair[t][:, S:], ACT.Ln, bias=0.3)
+
+        def log_v(t):
+            nc.scalar.activation(pair[t][:, :S], sig_v[t][:], ACT.Ln, bias=TINY)
+
+        def logit_sat(t):
+            nc.vector.tensor_tensor(sat_logit[t][:], conc_win[t][:, :S], log_km[t][:], ALU.subtract)
+
+        def logit_inh(t):
+            nc.vector.tensor_tensor(inh_logit[:, t, :], conc_win[t][:].indirect(prev_list[:]), log_km[t][:], ALU.subtract)
+
+        softplus_pair(0)
+        for t in range(1, PACK):
+            softplus_pair(t)
+            logs(t - 1)
+            log_v(t - 1)
+        logs(PACK - 1)
+        log_v(PACK - 1)
+        for t in range(PACK):
+            logit_sat(t)
+            logit_inh(t)
+
+        for t in range(PACK):
+            sat = pair[PACK - 1][:, S:] if t == 0 else sat_logit[t - 1][:]
+            nc.scalar.activation(sat, sat_logit[t][:], ACT.Sigmoid)
+            nc.vector.scalar_tensor_tensor(pair[t][:, :S], pair[t][:, :S], -1.0, vmx[t][:], ALU.mult, ALU.max)
+            nc.vector.scalar_tensor_tensor(rate[:, t, :], pair[t][:, :S], gain[:, t : t + 1], sat, ALU.mult, ALU.mult)
+
+        chunks = S // CHUNK
+        inh = tiles("inh", chunks, [P, PACK, CHUNK], F32)
+        rate_prev = tiles("rate_prev", chunks, [P, PACK, CHUNK], F32)
+        hid = tiles("hid", chunks, [P, CHUNK, PACK], BF16)
+        hid_codes = tiles("hid_codes", chunks, [P, CHUNK], U32)
+        hid_scales = tiles("hid_scales", chunks, [P, CHUNK], U8)
+        result = tiles("result", chunks, [P, CHUNK], F32)
+        for c in range(chunks):
+            cols = slice(c * CHUNK, (c + 1) * CHUNK)
+            nc.scalar.activation(inh[c][:], inh_logit[:, :, cols], ACT.Sigmoid, scale=-1.0)
+            for t in range(PACK):
+                nc.scalar.activation(
+                    rate_prev[c][:, t, :],
+                    rate[:, t, :].indirect(prev_list[:, c * CHUNK // 16 : (c + 1) * CHUNK // 16]),
+                    ACT.Copy,
+                )
+            flat_prev = rate_prev[c][:].rearrange("p t n -> p (t n)")
+            nc.vector.scalar_tensor_tensor(flat_prev, flat_prev, -0.6, inh[c][:].rearrange("p t n -> p (t n)"), ALU.mult, ALU.mult)
+            nc.vector.tensor_tensor(
+                hid[c][:], rate[:, :, cols].rearrange("p t n -> p n t"), rate_prev[c][:].rearrange("p t n -> p n t"), ALU.add
+            )
+            nc.vector.quantize_mx(
+                out=hid_codes[c][:].bitcast(FP8X4), scales=hid_scales[c][:], in_=hid[c][:].rearrange("p n t -> p (n t)")
+            )
+            acc = psum.tile([P, CHUNK], F32, name="acc%d" % c, tag="a%d" % c)
+            nc.tensor.matmul_mx(
+                out=acc[:],
+                lhsT=w4_codes[:].bitcast(FP4X4),
+                lhsT_scale=w_raw_scales[:, 3 * H :],
+                rhs=hid_codes[c][:].bitcast(FP8X4),
+                rhs_scale=hid_scales[c][:],
+                start=True,
+                stop=True,
+            )
+            nc.scalar.copy(result[c][:], acc[:])
+            nc.sync.dma_start(out[:, cols], result[c][:])

@@ -33,36 +33,25 @@ def tile_picked_yumfpk_wash_p_kernel(
         def tiles(name, count, shape, dtype):
             return [held.tile(shape, dtype, name="%s%d" % (name, i), align_bytes=64) for i in range(count)]
 
-        def load_scale_rows(dst, src, last_queue=nc.sync):
+        def load_scale_rows(dst, src):
             for q in range(4):
-                queue = last_queue if q == 3 else nc.sync
-                queue.dma_start(dst[32 * q : 32 * q + 4, :].bitcast(I32), src[0, 4 * q : 4 * q + 4, :].bitcast(I32))
+                nc.sync.dma_start(dst[32 * q : 32 * q + 4, :].bitcast(I32), src[0, 4 * q : 4 * q + 4, :].bitcast(I32))
 
         offs_list = held.tile([P, S // 16], U16, name="offs_list")
         prev_list = held.tile([P, S // 16], U16, name="prev_list")
         x_table = held.tile([P, T], U32, name="x_table", align_bytes=64)
         x_table_scales = held.tile([P, T], U8, name="x_table_scales", tag="scales_then_gain", align_bytes=64)
-        w_raw_scales = held.tile([P, 3 * H + N], U8, name="w_raw_scales", align_bytes=64)
+        w1_raw = held.tile([P, 2 * H], U8, name="w1_raw", tag="w_raw", align_bytes=64)
+        w1_raw_scales = held.tile([P, H], U8, name="w1_raw_scales", align_bytes=64)
 
         nc.vector.memset(x_table_scales[:].bitcast(I32), 0)
-        nc.gpsimd.memset(w_raw_scales[:].bitcast(I32), 0)
-
-        words_in = (w1_words, w3_words, w2_words)
-        scales_in = (w1_scales, w3_scales, w2_scales)
-        def load_words(name, src):
-            raw = held.tile([P, src.shape[2]], U8, name=name, tag="w_raw", align_bytes=64)
-            nc.sync.dma_start(raw[:].bitcast(I32), src[0].bitcast(I32))
-            return raw
-
+        nc.vector.memset(w1_raw_scales[:].bitcast(I32), 0)
         nc.sync.dma_start(offs_list[:], offs)
-        nc.sync.dma_start(prev_list[:], prev)
-        first_raw = load_words("w_raw0", words_in[0])
-        nc.sync.dma_start(x_table[:].bitcast(I32), x_words[0].rearrange("p n t -> p (n t)").bitcast(I32))
+        nc.scalar.dma_start(w1_raw[:].bitcast(I32), w1_words[0].bitcast(I32))
+        nc.scalar.dma_start(x_table[:].bitcast(I32), x_words[0].rearrange("p n t -> p (n t)").bitcast(I32))
         load_scale_rows(x_table_scales[:], x_scales)
-        load_scale_rows(w_raw_scales[:, :H], scales_in[0], last_queue=nc.gpsimd)
-        for i in (1, 2):
-            load_scale_rows(w_raw_scales[:, i * H : (i + 1) * H], scales_in[i])
-        load_scale_rows(w_raw_scales[:, 3 * H :], w4_scales)
+        load_scale_rows(w1_raw_scales[:], w1_scales)
+        nc.sync.dma_start(prev_list[:], prev)
 
         w_codes = tiles("w_codes", 3, [P, 2 * H], U8)
         w_scales = tiles("w_scales", 3, [P, H], U8)
@@ -70,25 +59,34 @@ def tile_picked_yumfpk_wash_p_kernel(
         def deal_words(i, raw):
             nc.vector.tensor_copy(
                 w_codes[i][:].rearrange("p (t m b) -> p t m b", t=PACK, b=2),
-                raw[:].rearrange("p (m t b) -> p t m b", t=PACK, b=2),
+                raw.rearrange("p (m t b) -> p t m b", t=PACK, b=2),
             )
 
-        def deal_scales(i):
+        def deal_scales(i, raw):
             nc.vector.tensor_copy(
                 w_scales[i][:].rearrange("p (t m) -> p t m", t=PACK),
-                w_raw_scales[:, i * H : (i + 1) * H].rearrange("p (m t) -> p t m", t=PACK),
+                raw.rearrange("p (m t) -> p t m", t=PACK),
             )
 
         x_codes = held.tile([P, S], U32, name="x_codes", align_bytes=64)
         x_picked_scales = held.tile([P, S], U8, name="x_picked_scales", align_bytes=64)
-        deal_words(0, first_raw)
+        deal_words(0, w1_raw[:])
         nc.vector.tensor_copy(x_picked_scales[:], x_table_scales[:].indirect(offs_list[:]))
+        deal_scales(0, w1_raw_scales[:])
         nc.vector.tensor_copy(x_codes[:], x_table[:].indirect(offs_list[:]))
-        deal_scales(0)
-        for i in (1, 2):
-            deal_words(i, load_words("w_raw%d" % i, words_in[i]))
-            deal_scales(i)
-        w4_codes = load_words("w4_codes", w4_words)
+
+        later = held.tile([P, 3 * (2 * H + N)], U8, name="later", tag="w_raw", align_bytes=64)
+        w3_raw, w2_raw, w4_codes = later[:, : 2 * H], later[:, 2 * H : 4 * H], later[:, 4 * H : 4 * H + 2 * N]
+        later_scales = later[:, 4 * H + 2 * N :]
+        w3_raw_scales, w2_raw_scales, w4_plane = later_scales[:, :H], later_scales[:, H : 2 * H], later_scales[:, 2 * H :]
+        nc.vector.memset(later_scales.bitcast(I32), 0)
+        for words, words_in, plane, plane_in in (
+            (w3_raw, w3_words, w3_raw_scales, w3_scales),
+            (w2_raw, w2_words, w2_raw_scales, w2_scales),
+            (w4_codes, w4_words, w4_plane, w4_scales),
+        ):
+            nc.sync.dma_start(words.bitcast(I32), words_in[0].bitcast(I32))
+            load_scale_rows(plane, plane_in)
         gain = held.tile([P, PACK], F32, name="gain", tag="scales_then_gain", align_bytes=64)
         nc.sync.dma_start(gain[:], unit.rearrange("(p t) o -> p (t o)", t=PACK))
 
@@ -117,6 +115,12 @@ def tile_picked_yumfpk_wash_p_kernel(
             bank = product(0, t, "a")
             nc.scalar.activation(pair[t][:, :S], bank[:], ACT.Sigmoid, scale=-1.0)
             nc.vector.tensor_scalar_max(conc_win[t][:, S:], bank[:], TINY)
+            if t == 0:
+                deal_words(1, w3_raw)
+                deal_scales(1, w3_raw_scales)
+            if t == 1:
+                deal_words(2, w2_raw)
+                deal_scales(2, w2_raw_scales)
         vmx = []
         for t in range(PACK):
             vmx.append(product(1, t, "b"))
@@ -180,7 +184,10 @@ def tile_picked_yumfpk_wash_p_kernel(
             flat_prev = rate_prev[c][:].rearrange("p t n -> p (t n)")
             nc.vector.scalar_tensor_tensor(flat_prev, flat_prev, -0.6, inh[c][:].rearrange("p t n -> p (t n)"), ALU.mult, ALU.mult)
             nc.vector.tensor_tensor(
-                hid[c][:], rate[:, :, cols].rearrange("p t n -> p n t"), rate_prev[c][:].rearrange("p t n -> p n t"), ALU.add
+                hid[c][:].rearrange("p (g i) t -> p g t i", i=4),
+                rate[:, :, cols].rearrange("p t (g i) -> p g t i", i=4),
+                rate_prev[c][:].rearrange("p t (g i) -> p g t i", i=4),
+                ALU.add,
             )
             nc.vector.quantize_mx(
                 out=hid_codes[c][:].bitcast(FP8X4), scales=hid_scales[c][:], in_=hid[c][:].rearrange("p n t -> p (n t)")
@@ -188,8 +195,8 @@ def tile_picked_yumfpk_wash_p_kernel(
             acc = psum.tile([P, CHUNK], F32, name="acc%d" % c, tag="a%d" % c)
             nc.tensor.matmul_mx(
                 out=acc[:],
-                lhsT=w4_codes[:].bitcast(FP4X4),
-                lhsT_scale=w_raw_scales[:, 3 * H :],
+                lhsT=w4_codes.bitcast(FP4X4),
+                lhsT_scale=w4_plane,
                 rhs=hid_codes[c][:].bitcast(FP8X4),
                 rhs_scale=hid_scales[c][:],
                 start=True,

@@ -16,7 +16,7 @@ ACT = mybir.ActivationFunctionType
 P = 128
 PACK = 4
 K, T, S, N, H = 512, 2048, 512, 128, 512
-CHUNK = 128
+EARLY = 256
 TINY = 1e-18
 FLOPS = 2 * K * H * S * 3 + 2 * H * N * S
 
@@ -103,17 +103,19 @@ def tile_picked_yumfpk_wash_p_kernel(
             )
             return bank
 
-        pair = tiles("pair", PACK, [P, 2 * S], F32)
+        pair = held.tile([P, PACK, 2 * S], F32, name="pair", align_bytes=64)
         conc_win = tiles("conc_win", PACK, [P, 2 * S], F32)
-        sig_v = tiles("sig_v", PACK, [P, S], F32)
+        sig_v = held.tile([P, PACK, S], F32, name="sig_v", align_bytes=64)
         log_km = tiles("log_km", PACK, [P, S], F32)
         sat_logit = tiles("sat_logit", PACK, [P, S], F32)
-        inh_logit = held.tile([P, PACK, S], F32, name="inh_logit", align_bytes=64)
+        inh_logit = held.tile([P, PACK, EARLY], F32, name="inh_logit", align_bytes=64)
         rate = held.tile([P, PACK, S], F32, name="rate", align_bytes=64)
+        last = PACK - 1
+        CHUNKS = [slice(0, 256), slice(256, 384), slice(384, 512)]
 
         for t in range(PACK):
             bank = product(0, t, "a")
-            nc.scalar.activation(pair[t][:, :S], bank[:], ACT.Sigmoid, scale=-1.0)
+            nc.scalar.activation(pair[:, t, :S], bank[:], ACT.Sigmoid, scale=-1.0)
             nc.vector.tensor_scalar_max(conc_win[t][:, S:], bank[:], TINY)
             if t == 0:
                 deal_words(1, w3_raw)
@@ -124,83 +126,81 @@ def tile_picked_yumfpk_wash_p_kernel(
         vmx = []
         for t in range(PACK):
             vmx.append(product(1, t, "b"))
-            nc.scalar.activation(sig_v[t][:], vmx[t][:], ACT.Sigmoid, scale=-1.0)
+            nc.scalar.activation(sig_v[:, t, :], vmx[t][:], ACT.Sigmoid, scale=-1.0)
         vd = []
         for t in range(PACK):
             vd.append(product(2, t, "a"))
-            nc.scalar.activation(pair[t][:, S:], vd[t][:], ACT.Sigmoid, scale=-1.0)
+            nc.scalar.activation(pair[:, t, S:], vd[t][:], ACT.Sigmoid, scale=-1.0)
 
         def softplus_pair(t):
-            nc.scalar.activation(pair[t][:], pair[t][:], ACT.Ln, bias=TINY)
-            nc.vector.scalar_tensor_tensor(conc_win[t][:, S:], pair[t][:, :S], -1.0, conc_win[t][:, S:], ALU.mult, ALU.max)
-            nc.vector.scalar_tensor_tensor(pair[t][:, S:], pair[t][:, S:], -1.0, vd[t][:], ALU.mult, ALU.max)
+            nc.scalar.activation(pair[:, t, :], pair[:, t, :], ACT.Ln, bias=TINY)
+            nc.vector.scalar_tensor_tensor(conc_win[t][:, S:], pair[:, t, :S], -1.0, conc_win[t][:, S:], ALU.mult, ALU.max)
+            nc.vector.scalar_tensor_tensor(pair[:, t, S:], pair[:, t, S:], -1.0, vd[t][:], ALU.mult, ALU.max)
 
         def logs(t):
             nc.scalar.activation(conc_win[t][:, :S], conc_win[t][:, S:], ACT.Ln)
-            nc.scalar.activation(log_km[t][:], pair[t][:, S:], ACT.Ln, bias=0.3)
+            nc.scalar.activation(log_km[t][:], pair[:, t, S:], ACT.Ln, bias=0.3)
 
-        def log_v(t):
-            nc.scalar.activation(pair[t][:, :S], sig_v[t][:], ACT.Ln, bias=TINY)
+        def log_v(t0):
+            nc.scalar.activation(pair[:, t0 : t0 + 2, :S], sig_v[:, t0 : t0 + 2, :], ACT.Ln, bias=TINY)
 
-        def logit_sat(t):
-            nc.vector.tensor_tensor(sat_logit[t][:], conc_win[t][:, :S], log_km[t][:], ALU.subtract)
+        def places(cols):
+            return prev_list[:, cols.start // 16 : cols.stop // 16]
 
-        def logit_inh(t):
-            nc.vector.tensor_tensor(inh_logit[:, t, :], conc_win[t][:].indirect(prev_list[:]), log_km[t][:], ALU.subtract)
+        def logit_inh(dst, t, cols):
+            nc.vector.tensor_tensor(dst, conc_win[t][:].indirect(places(cols)), log_km[t][:, cols], ALU.subtract)
 
         softplus_pair(0)
         for t in range(1, PACK):
             softplus_pair(t)
             logs(t - 1)
-            log_v(t - 1)
-        logs(PACK - 1)
-        log_v(PACK - 1)
+        log_v(0)
+        logs(last)
+        log_v(2)
         for t in range(PACK):
-            logit_sat(t)
-            logit_inh(t)
+            nc.vector.tensor_tensor(sat_logit[t][:], conc_win[t][:, :S], log_km[t][:], ALU.subtract)
+            logit_inh(inh_logit[:, t, :], t, slice(0, EARLY))
+        for t in range(PACK):
+            nc.vector.scalar_tensor_tensor(pair[:, t, :S], pair[:, t, :S], -1.0, vmx[t][:], ALU.mult, ALU.max)
 
         for t in range(PACK):
-            sat = pair[PACK - 1][:, S:] if t == 0 else sat_logit[t - 1][:]
+            sat = pair[:, last, S:] if t in (0, last) else sat_logit[t - 1][:]
             nc.scalar.activation(sat, sat_logit[t][:], ACT.Sigmoid)
-            nc.vector.scalar_tensor_tensor(pair[t][:, :S], pair[t][:, :S], -1.0, vmx[t][:], ALU.mult, ALU.max)
-            nc.vector.scalar_tensor_tensor(rate[:, t, :], pair[t][:, :S], gain[:, t : t + 1], sat, ALU.mult, ALU.mult)
+            nc.vector.scalar_tensor_tensor(rate[:, t, :], pair[:, t, :S], gain[:, t : t + 1], sat, ALU.mult, ALU.mult)
+        late_logit = pair[:, last, :].rearrange("p (t n) -> p t n", t=PACK)
+        for t in range(PACK):
+            logit_inh(late_logit[:, t, :], t, slice(EARLY, S))
 
-        chunks = S // CHUNK
-        inh = tiles("inh", chunks, [P, PACK, CHUNK], F32)
-        rate_prev = tiles("rate_prev", chunks, [P, PACK, CHUNK], F32)
-        hid = tiles("hid", chunks, [P, CHUNK, PACK], BF16)
-        hid_codes = tiles("hid_codes", chunks, [P, CHUNK], U32)
-        hid_scales = tiles("hid_scales", chunks, [P, CHUNK], U8)
-        result = tiles("result", chunks, [P, CHUNK], F32)
-        for c in range(chunks):
-            cols = slice(c * CHUNK, (c + 1) * CHUNK)
-            nc.scalar.activation(inh[c][:], inh_logit[:, :, cols], ACT.Sigmoid, scale=-1.0)
+        for c, cols in enumerate(CHUNKS):
+            width = cols.stop - cols.start
+            inh = held.tile([P, PACK, width], F32, name="inh%d" % c, align_bytes=64)
+            rate_prev = held.tile([P, PACK, width], F32, name="rate_prev%d" % c, align_bytes=64)
+            hid = held.tile([P, width, PACK], BF16, name="hid%d" % c, align_bytes=64)
+            hid_codes = held.tile([P, width], U32, name="hid_codes%d" % c, align_bytes=64)
+            hid_scales = held.tile([P, width], U8, name="hid_scales%d" % c, align_bytes=64)
+            result = held.tile([P, width], F32, name="result%d" % c, align_bytes=64)
+            logits = inh_logit[:, :, cols] if cols.stop <= EARLY else late_logit[:, :, cols.start - EARLY : cols.stop - EARLY]
+            nc.scalar.activation(inh[:], logits, ACT.Sigmoid, scale=-1.0)
             for t in range(PACK):
-                nc.scalar.activation(
-                    rate_prev[c][:, t, :],
-                    rate[:, t, :].indirect(prev_list[:, c * CHUNK // 16 : (c + 1) * CHUNK // 16]),
-                    ACT.Copy,
-                )
-            flat_prev = rate_prev[c][:].rearrange("p t n -> p (t n)")
-            nc.vector.scalar_tensor_tensor(flat_prev, flat_prev, -0.6, inh[c][:].rearrange("p t n -> p (t n)"), ALU.mult, ALU.mult)
+                nc.scalar.activation(rate_prev[:, t, :], rate[:, t, :].indirect(places(cols)), ACT.Copy)
+            flat_prev = rate_prev[:].rearrange("p t n -> p (t n)")
+            nc.vector.scalar_tensor_tensor(flat_prev, flat_prev, -0.6, inh[:].rearrange("p t n -> p (t n)"), ALU.mult, ALU.mult)
             nc.vector.tensor_tensor(
-                hid[c][:].rearrange("p (g i) t -> p g t i", i=4),
+                hid[:].rearrange("p (g i) t -> p g t i", i=4),
                 rate[:, :, cols].rearrange("p t (g i) -> p g t i", i=4),
-                rate_prev[c][:].rearrange("p t (g i) -> p g t i", i=4),
+                rate_prev[:].rearrange("p t (g i) -> p g t i", i=4),
                 ALU.add,
             )
-            nc.vector.quantize_mx(
-                out=hid_codes[c][:].bitcast(FP8X4), scales=hid_scales[c][:], in_=hid[c][:].rearrange("p n t -> p (n t)")
-            )
-            acc = psum.tile([P, CHUNK], F32, name="acc%d" % c, tag="a%d" % c)
+            nc.vector.quantize_mx(out=hid_codes[:].bitcast(FP8X4), scales=hid_scales[:], in_=hid[:].rearrange("p n t -> p (n t)"))
+            acc = psum.tile([P, width], F32, name="acc%d" % c, tag="a%d" % c)
             nc.tensor.matmul_mx(
                 out=acc[:],
                 lhsT=w4_codes.bitcast(FP4X4),
                 lhsT_scale=w4_plane,
-                rhs=hid_codes[c][:].bitcast(FP8X4),
-                rhs_scale=hid_scales[c][:],
+                rhs=hid_codes[:].bitcast(FP8X4),
+                rhs_scale=hid_scales[:],
                 start=True,
                 stop=True,
             )
-            nc.scalar.copy(result[c][:], acc[:])
-            nc.sync.dma_start(out[:, cols], result[c][:])
+            nc.scalar.copy(result[:], acc[:])
+            nc.sync.dma_start(out[:, cols], result[:])

@@ -111,7 +111,7 @@ def tile_picked_yumfpk_wash_p_kernel(
         inh_logit = held.tile([P, PACK, EARLY], F32, name="inh_logit", align_bytes=64)
         rate = held.tile([P, PACK, S], F32, name="rate", align_bytes=64)
         last = PACK - 1
-        CHUNKS = [slice(0, 256), slice(256, 384), slice(384, 512)]
+        CHUNKS = [slice(c, c + 128) for c in range(0, S, 128)]
 
         for t in range(PACK):
             bank = product(0, t, "a")

from contextlib import ExitStack

import concourse.mybir as mybir

F32 = mybir.dt.float32
BF16 = mybir.dt.bfloat16
I32 = mybir.dt.int32
U32 = mybir.dt.uint32
U16 = mybir.dt.uint16
U8 = mybir.dt.uint8
FP8X4 = mybir.dt.float8_e4m3fn_x4
FP4X4 = mybir.dt.float4_e2m1fn_x4
ALU = mybir.AluOpType
ACT = mybir.ActivationFunctionType

P = 128
PACK = 4
K, T, S, N, H = 512, 2048, 512, 128, 512
EARLY = 256
TINY = 1e-18
FLOPS = 2 * K * H * S * 3 + 2 * H * N * S


def tile_picked_yumfpk_wash_p_kernel(
    tc, x_words, x_scales, w1_words, w1_scales, w2_words, w2_scales, w3_words, w3_scales,
    unit, w4_words, w4_scales, offs, prev, out,
):
    nc = tc.nc
    with ExitStack() as ctx:
        held = ctx.enter_context(tc.tile_pool(name="held", bufs=1))
        psum = ctx.enter_context(tc.psum_pool(name="psum", bufs=1))

        def tiles(name, count, shape, dtype):
            return [held.tile(shape, dtype, name="%s%d" % (name, i), align_bytes=64) for i in range(count)]

        def load_scale_rows(dst, src):
            for q in range(4):
                nc.sync.dma_start(dst[32 * q : 32 * q + 4, :].bitcast(I32), src[0, 4 * q : 4 * q + 4, :].bitcast(I32))

        offs_list = held.tile([P, S // 16], U16, name="offs_list")
        prev_list = held.tile([P, S // 16], U16, name="prev_list")
        x_table = held.tile([P, T], U32, name="x_table", align_bytes=64)
        x_table_scales = held.tile([P, T], U8, name="x_table_scales", tag="scales_then_gain", align_bytes=64)
        w1_raw = held.tile([P, 2 * H], U8, name="w1_raw", tag="w_raw", align_bytes=64)
        w1_raw_scales = held.tile([P, H], U8, name="w1_raw_scales", align_bytes=64)

        nc.vector.memset(x_table_scales[:].bitcast(I32), 0)
        nc.vector.memset(w1_raw_scales[:].bitcast(I32), 0)
        nc.sync.dma_start(offs_list[:], offs)
        nc.scalar.dma_start(w1_raw[:].bitcast(I32), w1_words[0].bitcast(I32))
        nc.scalar.dma_start(x_table[:].bitcast(I32), x_words[0].rearrange("p n t -> p (n t)").bitcast(I32))
        load_scale_rows(x_table_scales[:], x_scales)
        load_scale_rows(w1_raw_scales[:], w1_scales)
        nc.sync.dma_start(prev_list[:], prev)

        w_codes = tiles("w_codes", 3, [P, 2 * H], U8)
        w_scales = tiles("w_scales", 3, [P, H], U8)

        def deal_words(i, raw):
            nc.vector.tensor_copy(
                w_codes[i][:].rearrange("p (t m b) -> p t m b", t=PACK, b=2),
                raw.rearrange("p (m t b) -> p t m b", t=PACK, b=2),
            )

        def deal_scales(i, raw):
            nc.vector.tensor_copy(
                w_scales[i][:].rearrange("p (t m) -> p t m", t=PACK),
                raw.rearrange("p (m t) -> p t m", t=PACK),
            )

        x_codes = held.tile([P, S], U32, name="x_codes", align_bytes=64)
        x_picked_scales = held.tile([P, S], U8, name="x_picked_scales", align_bytes=64)
        deal_words(0, w1_raw[:])
        nc.vector.tensor_copy(x_picked_scales[:], x_table_scales[:].indirect(offs_list[:]))
        deal_scales(0, w1_raw_scales[:])
        nc.vector.tensor_copy(x_codes[:], x_table[:].indirect(offs_list[:]))

        later = held.tile([P, 3 * (2 * H + N)], U8, name="later", tag="w_raw", align_bytes=64)
        w3_raw, w2_raw, w4_codes = later[:, : 2 * H], later[:, 2 * H : 4 * H], later[:, 4 * H : 4 * H + 2 * N]
        later_scales = later[:, 4 * H + 2 * N :]
        w3_raw_scales, w2_raw_scales, w4_plane = later_scales[:, :H], later_scales[:, H : 2 * H], later_scales[:, 2 * H :]
        nc.vector.memset(later_scales.bitcast(I32), 0)
        for words, words_in, plane, plane_in in (
            (w3_raw, w3_words, w3_raw_scales, w3_scales),
            (w2_raw, w2_words, w2_raw_scales, w2_scales),
            (w4_codes, w4_words, w4_plane, w4_scales),
        ):
            nc.sync.dma_start(words.bitcast(I32), words_in[0].bitcast(I32))
            load_scale_rows(plane, plane_in)
        gain = held.tile([P, PACK], F32, name="gain", tag="scales_then_gain", align_bytes=64)
        nc.sync.dma_start(gain[:], unit.rearrange("(p t) o -> p (t o)", t=PACK))

        def product(i, t, tag):
            bank = psum.tile([P, S], F32, name="pre%d_%d" % (i, t), tag="%s%d" % (tag, t))
            nc.tensor.matmul_mx(
                out=bank[:],
                lhsT=w_codes[i][:, 2 * P * t : 2 * P * (t + 1)].bitcast(FP4X4),
                lhsT_scale=w_scales[i][:, P * t : P * (t + 1)],
                rhs=x_codes[:].bitcast(FP8X4),
                rhs_scale=x_picked_scales[:],
                start=True,
                stop=True,
            )
            return bank

        pair = held.tile([P, PACK, 2 * S], F32, name="pair", align_bytes=64)
        conc_win = tiles("conc_win", PACK, [P, 2 * S], F32)
        sig_v = held.tile([P, PACK, S], F32, name="sig_v", align_bytes=64)
        log_km = tiles("log_km", PACK, [P, S], F32)
        sat_logit = tiles("sat_logit", PACK, [P, S], F32)
        inh_logit = held.tile([P, PACK, EARLY], F32, name="inh_logit", align_bytes=64)
        rate = held.tile([P, PACK, S], F32, name="rate", align_bytes=64)
        last = PACK - 1
        CHUNKS = [slice(c, c + 128) for c in range(0, S, 128)]

        for t in range(PACK):
            bank = product(0, t, "a")
            nc.scalar.activation(pair[:, t, :S], bank[:], ACT.Sigmoid, scale=-1.0)
            nc.vector.tensor_scalar_max(conc_win[t][:, S:], bank[:], TINY)
            if t == 0:
                deal_words(1, w3_raw)
                deal_scales(1, w3_raw_scales)
            if t == 1:
                deal_words(2, w2_raw)
                deal_scales(2, w2_raw_scales)
        vmx = []
        for t in range(PACK):
            vmx.append(product(1, t, "b"))
            nc.scalar.activation(sig_v[:, t, :], vmx[t][:], ACT.Sigmoid, scale=-1.0)
        vd = []
        for t in range(PACK):
            vd.append(product(2, t, "a"))
            nc.scalar.activation(pair[:, t, S:], vd[t][:], ACT.Sigmoid, scale=-1.0)

        def softplus_pair(t):
            nc.scalar.activation(pair[:, t, :], pair[:, t, :], ACT.Ln, bias=TINY)
            nc.vector.scalar_tensor_tensor(conc_win[t][:, S:], pair[:, t, :S], -1.0, conc_win[t][:, S:], ALU.mult, ALU.max)
            nc.vector.scalar_tensor_tensor(pair[:, t, S:], pair[:, t, S:], -1.0, vd[t][:], ALU.mult, ALU.max)

        def logs(t):
            nc.scalar.activation(conc_win[t][:, :S], conc_win[t][:, S:], ACT.Ln)
            nc.scalar.activation(log_km[t][:], pair[:, t, S:], ACT.Ln, bias=0.3)

        def log_v(t0):
            nc.scalar.activation(pair[:, t0 : t0 + 2, :S], sig_v[:, t0 : t0 + 2, :], ACT.Ln, bias=TINY)

        def places(cols):
            return prev_list[:, cols.start // 16 : cols.stop // 16]

        def logit_inh(dst, t, cols):
            nc.vector.tensor_tensor(dst, conc_win[t][:].indirect(places(cols)), log_km[t][:, cols], ALU.subtract)

        softplus_pair(0)
        for t in range(1, PACK):
            softplus_pair(t)
            logs(t - 1)
        log_v(0)
        logs(last)
        log_v(2)
        for t in range(PACK):
            nc.vector.tensor_tensor(sat_logit[t][:], conc_win[t][:, :S], log_km[t][:], ALU.subtract)
            logit_inh(inh_logit[:, t, :], t, slice(0, EARLY))
        for t in range(PACK):
            nc.vector.scalar_tensor_tensor(pair[:, t, :S], pair[:, t, :S], -1.0, vmx[t][:], ALU.mult, ALU.max)

        for t in range(PACK):
            sat = pair[:, last, S:] if t in (0, last) else sat_logit[t - 1][:]
            nc.scalar.activation(sat, sat_logit[t][:], ACT.Sigmoid)
            nc.vector.scalar_tensor_tensor(rate[:, t, :], pair[:, t, :S], gain[:, t : t + 1], sat, ALU.mult, ALU.mult)
        late_logit = pair[:, last, :].rearrange("p (t n) -> p t n", t=PACK)
        for t in range(PACK):
            logit_inh(late_logit[:, t, :], t, slice(EARLY, S))

        for c, cols in enumerate(CHUNKS):
            width = cols.stop - cols.start
            inh = held.tile([P, PACK, width], F32, name="inh%d" % c, align_bytes=64)
            rate_prev = held.tile([P, PACK, width], F32, name="rate_prev%d" % c, align_bytes=64)
            hid = held.tile([P, width, PACK], BF16, name="hid%d" % c, align_bytes=64)
            hid_codes = held.tile([P, width], U32, name="hid_codes%d" % c, align_bytes=64)
            hid_scales = held.tile([P, width], U8, name="hid_scales%d" % c, align_bytes=64)
            result = held.tile([P, width], F32, name="result%d" % c, align_bytes=64)
            logits = inh_logit[:, :, cols] if cols.stop <= EARLY else late_logit[:, :, cols.start - EARLY : cols.stop - EARLY]
            nc.scalar.activation(inh[:], logits, ACT.Sigmoid, scale=-1.0)
            for t in range(PACK):
                nc.scalar.activation(rate_prev[:, t, :], rate[:, t, :].indirect(places(cols)), ACT.Copy)
            flat_prev = rate_prev[:].rearrange("p t n -> p (t n)")
            nc.vector.scalar_tensor_tensor(flat_prev, flat_prev, -0.6, inh[:].rearrange("p t n -> p (t n)"), ALU.mult, ALU.mult)
            nc.vector.tensor_tensor(
                hid[:].rearrange("p (g i) t -> p g t i", i=4),
                rate[:, :, cols].rearrange("p t (g i) -> p g t i", i=4),
                rate_prev[:].rearrange("p t (g i) -> p g t i", i=4),
                ALU.add,
            )
            nc.vector.quantize_mx(out=hid_codes[:].bitcast(FP8X4), scales=hid_scales[:], in_=hid[:].rearrange("p n t -> p (n t)"))
            acc = psum.tile([P, width], F32, name="acc%d" % c, tag="a%d" % c)
            nc.tensor.matmul_mx(
                out=acc[:],
                lhsT=w4_codes.bitcast(FP4X4),
                lhsT_scale=w4_plane,
                rhs=hid_codes[:].bitcast(FP8X4),
                rhs_scale=hid_scales[:],
                start=True,
                stop=True,
            )
            nc.scalar.copy(result[:], acc[:])
            nc.sync.dma_start(out[:, cols], result[:])
